import numpy as np
import ml_dtypes


def mxq(x, axis, fmt="e4m3"):
    dtype, down = {"e4m3": (ml_dtypes.float8_e4m3fn, 7), "e5m2": (ml_dtypes.float8_e5m2, 14)}[fmt]
    v = np.moveaxis(np.asarray(x, np.float32).astype(ml_dtypes.bfloat16).astype(np.float64), axis, -1)
    blocks = v.reshape(v.shape[:-1] + (-1, 32))
    amax = np.abs(blocks).max(-1, keepdims=True)
    byte = np.maximum(np.where(amax > 0, np.frexp(amax)[1] - 1 + 127, 0) - down, 1)
    scale = np.exp2(byte - 127.0)
    codes = (blocks / scale).astype(np.float32).astype(dtype).astype(np.float64)
    return np.moveaxis((codes * scale).reshape(v.shape), -1, axis)


WIDE = False


def mx_kscale(k):
    if not WIDE:
        return np.ones(k)
    levels = np.array([10, -10, 5, -5, 0])
    if k % 512:
        return np.exp2(np.random.permutation(np.resize(levels, k // 32))).repeat(32)
    a = np.empty((k // 512, 16))
    for p in range(k // 512):
        a[p, :8] = np.random.permutation(np.resize(levels, 8))
        for g in range(8):
            far = levels[np.abs(levels - a[p, g]) >= 10]
            a[p, g + 8] = far[np.random.randint(len(far))]
    return np.exp2(a.ravel()).repeat(32)


def f64(x):
    return np.asarray(x).astype(np.float64)


def striped(idx):
    return np.tile(np.asarray(idx).reshape(-1, 16).T, (8, 1)).astype(np.uint16)


def unstriped(offs):
    return offs[:16].T.reshape(-1).astype(np.int64)


E2M1 = np.array([0.0, 0.5, 1.0, 1.5, 2.0, 3.0, 4.0, 6.0, -0.0, -0.5, -1.0, -1.5, -2.0, -3.0, -4.0, -6.0])


def pack_weight(w, fmt):
    k, n = w.shape
    w = f64(np.asarray(w, np.float32).astype(ml_dtypes.bfloat16)).reshape(k // 32, 32, n)
    amax = np.abs(w).max(1)
    if fmt == "e4m3":
        byte = np.frexp(amax)[1] - 1 + 127 - 7
    else:
        mant, ex = np.frexp(amax / 6.0)
        byte = np.where(mant > 0.5, ex, ex - 1) + 127
    byte = np.clip(np.where(amax > 0, byte, 1), 1, 254)
    scaled = (w * np.exp2(127.0 - byte)[:, None, :]).reshape(k, n).astype(np.float32)
    by_word = np.ascontiguousarray(scaled.reshape(k // 512, 128, 4, n).transpose(0, 1, 3, 2))
    if fmt == "e4m3":
        words = by_word.astype(ml_dtypes.float8_e4m3fn).view(np.uint8)
    else:
        c = by_word.astype(ml_dtypes.float4_e2m1fn).view(np.uint8) & 0xF
        words = (c[..., 0::2] | (c[..., 1::2] << 4)).reshape(k // 512, 128, 2 * n)
    return np.ascontiguousarray(words), np.ascontiguousarray(byte.astype(np.uint8).reshape(k // 512, 16, n))


def unpack_weight(words, scales, fmt):
    g, _, n = scales.shape
    words = np.ascontiguousarray(words).reshape(g, 128, n, -1)
    if fmt == "e4m3":
        vals = words.view(ml_dtypes.float8_e4m3fn).astype(np.float64)
    else:
        nib = np.empty((g, 128, n, 4), np.uint8)
        nib[..., 0::2] = words & 0xF
        nib[..., 1::2] = words >> 4
        vals = E2M1[nib]
    vals = vals * np.repeat(np.exp2(scales.astype(np.float64) - 127.0), 8, axis=1)[..., None]
    return vals.transpose(0, 1, 3, 2).reshape(g * 512, n)


K, T, C, J, I = 1024, 1024, 1024, 512, 512


def setup_inputs():
    n = np.random.standard_normal
    idx = np.random.permutation(T)[:J]
    idx2 = np.random.permutation(C)[:I]
    fk = mx_kscale(K)
    xap = pack_weight(n((K, T)) * 0.03 * fk[:, None], "e4m3")
    return {
        "xa_words": xap[0],
        "xa_scales": xap[1],
        "wc": (n((K, C)) / fk[:, None]).astype(np.float32),
        "cb": np.tile(0.5 * n(C), (128, 1)).astype(np.float32),
        "offs": striped(idx),
        "offs2": striped(idx2),
    }


def reference(xa_words, xa_scales, wc, cb, offs, offs2):
    idx = unstriped(offs)
    idx2 = unstriped(offs2)
    xau = unpack_weight(xa_words, xa_scales, "e4m3")
    xaidxg = xau[:, idx]
    wcidx2q = mxq(f64(wc)[:, idx2], 0, "e4m3")
    a = xaidxg.T @ wcidx2q
    y = np.tanh(a + f64(cb)[:1][:, idx2])
    return y

@@ -1,0 +1,152 @@
+from contextlib import ExitStack
+
+import concourse.mybir as mybir
+from concourse.masks import make_identity
+
+K, T, C, J, I = 1024, 1024, 1024, 512, 512
+FLOPS = 2 * K * J * I
+BYTES = K * T + K * T // 32 + 4 * K * C + 4 * C + 2 * 2 * 128 * 32 + 4 * J * I
+
+F32 = mybir.dt.float32
+BF16 = mybir.dt.bfloat16
+I32 = mybir.dt.int32
+U32 = mybir.dt.uint32
+U16 = mybir.dt.uint16
+U8 = mybir.dt.uint8
+FP8X4 = mybir.dt.float8_e4m3fn_x4
+ADD = mybir.AluOpType.add
+TANH = mybir.ActivationFunctionType.Tanh
+
+P = 128
+HALF = 256
+
+
+def tile_list_picked_tokens_by_picked_classes_kernel(tc, xa_words, xa_scales, wc, cb, offs, offs2, out):
+    nc = tc.nc
+    with ExitStack() as ctx:
+        keep = ctx.enter_context(tc.tile_pool(name="keep", bufs=1))
+        psum = ctx.enter_context(tc.psum_pool(name="psum", bufs=1))
+
+        tok_list = keep.tile([P, J // 16], U16, name="tok_list")
+        cls_list = keep.tile([P, I // 16], U16, name="cls_list")
+        x_words = [keep.tile([P, T], I32, name=f"x_words{z}") for z in range(2)]
+        x_scales = keep.tile([P, T // 4], I32, name="x_scales")
+        cb_row = keep.tile([P, C], F32, name="cb_row")
+        ident = keep.tile([P, P], F32, name="ident")
+        warm = keep.tile([P, 8], F32, name="warm")
+        warm_out = keep.tile([P, 8], F32, name="warm_out")
+        raw = [[keep.tile([P, 2, C // 2], F32, name=f"raw{q}_{h}") for h in range(2)] for q in range(4)]
+        pairs = [keep.tile([P, C], F32, name=f"pairs{q}") for q in range(4)]
+
+        nc.gpsimd.memset(x_scales[:], 0)
+        nc.vector.memset(warm[:], 0.0)
+        nc.vector.memset(cb_row[0:P - 1, :], 0.0)
+        nc.scalar.activation(out=warm_out[:], in_=warm[:], func=TANH)
+
+        wc_rows = wc.rearrange("(z p u t) c -> z u p t c", z=2, u=2, t=2)
+
+        def load_wc(q, h):
+            nc.sync.dma_start(out=raw[q][h][:], in_=wc_rows[q // 2, q % 2][:, :, h * (C // 2):(h + 1) * (C // 2)])
+
+        def load_x(z):
+            nc.sync.dma_start(out=x_words[z][:], in_=xa_words[z].rearrange("p n t -> p (n t)").bitcast(I32))
+
+        nc.sync.dma_start(tok_list[:], offs)
+        load_x(0)
+        load_wc(0, 0)
+        sc32 = xa_scales.bitcast(I32)
+        for quad in range(4):
+            nc.sync.dma_start(out=x_scales[32 * quad:32 * quad + 8, :], in_=sc32[:, 4 * quad:4 * quad + 4, :])
+        nc.sync.dma_start(cls_list[:], offs2)
+        nc.sync.dma_start(out=cb_row[P - 1:P, :], in_=cb[0:1, :])
+        load_wc(0, 1)
+        for q in range(1, 4):
+            load_wc(q, 0)
+            load_wc(q, 1)
+        load_x(1)
+        make_identity(nc, ident[:])
+
+        def cast(q, h, eng):
+            dst = pairs[q][:].bitcast(BF16).rearrange("p (c t) -> p c t", t=2)[:, h * (C // 2):(h + 1) * (C // 2), :]
+            src = raw[q][h][:].rearrange("p t c -> p c t")
+            if eng == "scalar":
+                nc.scalar.copy(out=dst, in_=src)
+            else:
+                nc.vector.tensor_copy(out=dst, in_=src)
+
+        xg = [keep.tile([P, J], U32, name=f"xg{z}", align_bytes=64) for z in range(2)]
+        xsg = keep.tile([P, J], U8, name="xsg", align_bytes=64)
+        wq = [keep.tile([P, I], U32, name=f"wq{z}", align_bytes=64) for z in range(2)]
+        ws = [keep.tile([P, I], U8, name=f"ws{z}", align_bytes=64) for z in range(2)]
+        cbg = keep.tile([P, I], F32, name="cbg")
+        bcol = keep.tile([P, 4], F32, name="bcol")
+        bias = keep.tile([P, I], F32, name="bias")
+        g0 = keep.tile([P, 2, I], F32, name="g0")
+        il0 = keep.tile([P, I, 2], F32, name="il0", align_bytes=64)
+        g1 = [keep.tile([P, 2, HALF], F32, name=f"g1_{h}") for h in range(2)]
+        il1 = [keep.tile([P, HALF, 2], F32, name=f"il1_{h}", align_bytes=64) for h in range(2)]
+        acc = [psum.tile([P, I], F32, name=f"acc{b}") for b in range(4)]
+        ps1 = psum.tile([P, 4, P], F32, name="ps1")
+        ps2 = psum.tile([P, I], F32, name="ps2")
+
+        def half_list(lst, h):
+            return lst[:, h * (HALF // 16):(h + 1) * (HALF // 16)]
+
+        def multiply(z, b):
+            cols = slice(b * P, (b + 1) * P)
+            nc.tensor.matmul_mx(
+                out=acc[b][:],
+                lhsT=xg[z][:, cols].bitcast(FP8X4),
+                lhsT_scale=xsg[4 * z:P, cols],
+                rhs=wq[z][:].bitcast(FP8X4),
+                rhs_scale=ws[z][:],
+                start=(z == 0),
+                stop=(z == 1),
+            )
+
+        cast(0, 0, "scalar")
+        nc.vector.tensor_copy(out=xg[0][:], in_=x_words[0][:].bitcast(U32).indirect(tok_list[:]))
+        nc.vector.tensor_copy(out=xsg[:], in_=x_scales[:].bitcast(U8).indirect(tok_list[:]))
+        nc.vector.tensor_copy(out=cbg[:], in_=cb_row[:].indirect(cls_list[:]))
+        cast(0, 1, "scalar")
+        nc.vector.tensor_copy(out=g0[:, 0, :], in_=pairs[0][:].indirect(cls_list[:]))
+        for b in range(4):
+            nc.tensor.transpose(ps1[:, b, :], cbg[:, b * P:(b + 1) * P], ident[:])
+        nc.vector.tensor_copy(out=bcol[:], in_=ps1[:, :, P - 1])
+        for b in range(4):
+            nc.tensor.transpose(ps2[:, b * P:(b + 1) * P], bcol[:, b:b + 1].to_broadcast([P, P]), ident[:])
+        cast(1, 0, "scalar")
+        cast(1, 1, "scalar")
+        nc.vector.tensor_copy(out=g0[:, 1, :], in_=pairs[1][:].indirect(cls_list[:]))
+        nc.vector.tensor_copy(out=il0[:], in_=g0[:].rearrange("p u c -> p c u"))
+        nc.vector.tensor_copy(out=bias[:], in_=ps2[:])
+        nc.vector.quantize_mx(out=wq[0][:].bitcast(FP8X4), scales=ws[0][:],
+                              in_=il0[:].rearrange("p c u -> p (c u)").bitcast(BF16))
+        for b in range(4):
+            multiply(0, b)
+        cast(2, 0, "scalar")
+        cast(2, 1, "scalar")
+        for h in range(2):
+            nc.vector.tensor_copy(out=g1[h][:, 0, :], in_=pairs[2][:].indirect(half_list(cls_list, h)))
+        cast(3, 0, "scalar")
+        cast(3, 1, "vector")
+        for h in range(2):
+            nc.vector.tensor_copy(out=g1[h][:, 1, :], in_=pairs[3][:].indirect(half_list(cls_list, h)))
+            nc.scalar.copy(out=il1[h][:], in_=g1[h][:].rearrange("p u c -> p c u"))
+        nc.vector.tensor_copy(out=xg[1][:, 0:HALF], in_=x_words[1][:].bitcast(U32).indirect(half_list(tok_list, 0)))
+        for h in range(2):
+            cols = slice(h * HALF, (h + 1) * HALF)
+            nc.vector.quantize_mx(out=wq[1][:, cols].bitcast(FP8X4), scales=ws[1][:, cols],
+                                  in_=il1[h][:].rearrange("p c u -> p (c u)").bitcast(BF16))
+        nc.vector.tensor_copy(out=xg[1][:, HALF:J], in_=x_words[1][:].bitcast(U32).indirect(half_list(tok_list, 1)))
+        for b in range(4):
+            multiply(1, b)
+        for b in range(4):
+            parts = [slice(0, I)] if b < 3 else [slice(0, HALF), slice(HALF, I)]
+            for n, cols in enumerate(parts):
+                width = cols.stop - cols.start
+                pre = keep.tile([P, width], F32, name=f"pre{b}_{n}")
+                res = keep.tile([P, width], F32, name=f"res{b}_{n}")
+                nc.vector.tensor_tensor(out=pre[:], in0=acc[b][:, cols], in1=bias[:, cols], op=ADD)
+                nc.scalar.activation(out=res[:], in_=pre[:], func=TANH)
+                nc.sync.dma_start(out=out[b * P:(b + 1) * P, cols], in_=res[:])

@@ -35,7 +35,7 @@ def tile_list_picked_tokens_by_picked_classes_kernel(tc, xa_words, xa_scales, wc
         ident = keep.tile([P, P], F32, name="ident")
         warm = keep.tile([P, 8], F32, name="warm")
         warm_out = keep.tile([P, 8], F32, name="warm_out")
-        raw = [[keep.tile([P, 2, C // 2], F32, name=f"raw{q}_{h}") for h in range(2)] for q in range(4)]
+        raw = [[keep.tile([P, 2, C // 2], F32, name=f"raw{q}_{h}", tag=f"raw{q}_{h}") for h in range(2)] for q in range(4)]
         pairs = [keep.tile([P, C], F32, name=f"pairs{q}") for q in range(4)]
 
         nc.gpsimd.memset(x_scales[:], 0)
@@ -51,39 +51,39 @@ def tile_list_picked_tokens_by_picked_classes_kernel(tc, xa_words, xa_scales, wc
         def load_x(z):
             nc.sync.dma_start(out=x_words[z][:], in_=xa_words[z].rearrange("p n t -> p (n t)").bitcast(I32))
 
+        nc.sync.dma_start(cls_list[:], offs2)
         nc.sync.dma_start(tok_list[:], offs)
-        load_x(0)
+        nc.sync.dma_start(out=cb_row[P - 1:P, :], in_=cb[0:1, :])
         load_wc(0, 0)
+        load_x(0)
+        load_wc(0, 1)
         sc32 = xa_scales.bitcast(I32)
         for quad in range(4):
             nc.sync.dma_start(out=x_scales[32 * quad:32 * quad + 8, :], in_=sc32[:, 4 * quad:4 * quad + 4, :])
-        nc.sync.dma_start(cls_list[:], offs2)
-        nc.sync.dma_start(out=cb_row[P - 1:P, :], in_=cb[0:1, :])
-        load_wc(0, 1)
         for q in range(1, 4):
             load_wc(q, 0)
             load_wc(q, 1)
         load_x(1)
         make_identity(nc, ident[:])
 
-        def cast(q, h, eng):
-            dst = pairs[q][:].bitcast(BF16).rearrange("p (c t) -> p c t", t=2)[:, h * (C // 2):(h + 1) * (C // 2), :]
-            src = raw[q][h][:].rearrange("p t c -> p c t")
+        def cast(q, h, eng, lo=0, hi=C // 2):
+            dst = pairs[q][:].bitcast(BF16).rearrange("p (c t) -> p c t", t=2)[:, h * (C // 2) + lo:h * (C // 2) + hi, :]
+            src = raw[q][h][:, :, lo:hi].rearrange("p t c -> p c t")
             if eng == "scalar":
                 nc.scalar.copy(out=dst, in_=src)
             else:
                 nc.vector.tensor_copy(out=dst, in_=src)
 
-        xg = [keep.tile([P, J], U32, name=f"xg{z}", align_bytes=64) for z in range(2)]
+        xg0 = keep.tile([P, J], U32, name="xg0", align_bytes=64)
+        xg1a = keep.tile([P, HALF], U32, name="xg1a", align_bytes=64)
         xsg = keep.tile([P, J], U8, name="xsg", align_bytes=64)
         wq = [keep.tile([P, I], U32, name=f"wq{z}", align_bytes=64) for z in range(2)]
         ws = [keep.tile([P, I], U8, name=f"ws{z}", align_bytes=64) for z in range(2)]
         cbg = keep.tile([P, I], F32, name="cbg")
         bcol = keep.tile([P, 4], F32, name="bcol")
-        bias = keep.tile([P, I], F32, name="bias")
         g0 = keep.tile([P, 2, I], F32, name="g0")
-        il0 = keep.tile([P, I, 2], F32, name="il0", align_bytes=64)
-        g1 = [keep.tile([P, 2, HALF], F32, name=f"g1_{h}") for h in range(2)]
+        il0 = [keep.tile([P, HALF, 2], F32, name=f"il0_{h}", align_bytes=64) for h in range(2)]
+        g1 = [keep.tile([P, 2, HALF], F32, name=f"g1_{h}", tag=f"g1_{h}", align_bytes=64) for h in range(2)]
         il1 = [keep.tile([P, HALF, 2], F32, name=f"il1_{h}", align_bytes=64) for h in range(2)]
         acc = [psum.tile([P, I], F32, name=f"acc{b}") for b in range(4)]
         ps1 = psum.tile([P, 4, P], F32, name="ps1")
@@ -92,11 +92,11 @@ def tile_list_picked_tokens_by_picked_classes_kernel(tc, xa_words, xa_scales, wc
         def half_list(lst, h):
             return lst[:, h * (HALF // 16):(h + 1) * (HALF // 16)]
 
-        def multiply(z, b):
+        def multiply(z, b, words):
             cols = slice(b * P, (b + 1) * P)
             nc.tensor.matmul_mx(
                 out=acc[b][:],
-                lhsT=xg[z][:, cols].bitcast(FP8X4),
+                lhsT=words.bitcast(FP8X4),
                 lhsT_scale=xsg[4 * z:P, cols],
                 rhs=wq[z][:].bitcast(FP8X4),
                 rhs_scale=ws[z][:],
@@ -104,43 +104,48 @@ def tile_list_picked_tokens_by_picked_classes_kernel(tc, xa_words, xa_scales, wc
                 stop=(z == 1),
             )
 
-        cast(0, 0, "scalar")
-        nc.vector.tensor_copy(out=xg[0][:], in_=x_words[0][:].bitcast(U32).indirect(tok_list[:]))
-        nc.vector.tensor_copy(out=xsg[:], in_=x_scales[:].bitcast(U8).indirect(tok_list[:]))
         nc.vector.tensor_copy(out=cbg[:], in_=cb_row[:].indirect(cls_list[:]))
-        cast(0, 1, "scalar")
-        nc.vector.tensor_copy(out=g0[:, 0, :], in_=pairs[0][:].indirect(cls_list[:]))
+        cast(0, 0, "scalar")
         for b in range(4):
             nc.tensor.transpose(ps1[:, b, :], cbg[:, b * P:(b + 1) * P], ident[:])
         nc.vector.tensor_copy(out=bcol[:], in_=ps1[:, :, P - 1])
         for b in range(4):
             nc.tensor.transpose(ps2[:, b * P:(b + 1) * P], bcol[:, b:b + 1].to_broadcast([P, P]), ident[:])
+        nc.vector.tensor_copy(out=xg0[:], in_=x_words[0][:].bitcast(U32).indirect(tok_list[:]))
+        nc.vector.tensor_copy(out=xsg[:], in_=x_scales[:].bitcast(U8).indirect(tok_list[:]))
+        cast(0, 1, "scalar")
+        nc.vector.tensor_copy(out=g0[:, 0, :], in_=pairs[0][:].indirect(cls_list[:]))
         cast(1, 0, "scalar")
         cast(1, 1, "scalar")
         nc.vector.tensor_copy(out=g0[:, 1, :], in_=pairs[1][:].indirect(cls_list[:]))
-        nc.vector.tensor_copy(out=il0[:], in_=g0[:].rearrange("p u c -> p c u"))
-        nc.vector.tensor_copy(out=bias[:], in_=ps2[:])
-        nc.vector.quantize_mx(out=wq[0][:].bitcast(FP8X4), scales=ws[0][:],
-                              in_=il0[:].rearrange("p c u -> p (c u)").bitcast(BF16))
+        for h in range(2):
+            nc.vector.tensor_copy(out=il0[h][:], in_=g0[:, :, h * HALF:(h + 1) * HALF].rearrange("p u c -> p c u"))
+        for h in range(2):
+            cols = slice(h * HALF, (h + 1) * HALF)
+            nc.vector.quantize_mx(out=wq[0][:, cols].bitcast(FP8X4), scales=ws[0][:, cols],
+                                  in_=il0[h][:].rearrange("p c u -> p (c u)").bitcast(BF16))
         for b in range(4):
-            multiply(0, b)
+            multiply(0, b, xg0[:, b * P:(b + 1) * P])
         cast(2, 0, "scalar")
         cast(2, 1, "scalar")
         for h in range(2):
             nc.vector.tensor_copy(out=g1[h][:, 0, :], in_=pairs[2][:].indirect(half_list(cls_list, h)))
         cast(3, 0, "scalar")
         cast(3, 1, "vector")
+        bias = keep.tile([P, I], F32, name="bias", tag="raw3_0")
+        nc.scalar.copy(out=bias[:], in_=ps2[:])
         for h in range(2):
             nc.vector.tensor_copy(out=g1[h][:, 1, :], in_=pairs[3][:].indirect(half_list(cls_list, h)))
             nc.scalar.copy(out=il1[h][:], in_=g1[h][:].rearrange("p u c -> p c u"))
-        nc.vector.tensor_copy(out=xg[1][:, 0:HALF], in_=x_words[1][:].bitcast(U32).indirect(half_list(tok_list, 0)))
+        nc.vector.tensor_copy(out=xg1a[:], in_=x_words[1][:].bitcast(U32).indirect(half_list(tok_list, 0)))
         for h in range(2):
             cols = slice(h * HALF, (h + 1) * HALF)
             nc.vector.quantize_mx(out=wq[1][:, cols].bitcast(FP8X4), scales=ws[1][:, cols],
                                   in_=il1[h][:].rearrange("p c u -> p (c u)").bitcast(BF16))
-        nc.vector.tensor_copy(out=xg[1][:, HALF:J], in_=x_words[1][:].bitcast(U32).indirect(half_list(tok_list, 1)))
+        xg1b = keep.tile([P, HALF], U32, name="xg1b", tag="g1_1", align_bytes=64)
+        nc.vector.tensor_copy(out=xg1b[:], in_=x_words[1][:].bitcast(U32).indirect(half_list(tok_list, 1)))
         for b in range(4):
-            multiply(1, b)
+            multiply(1, b, (xg1a, xg1b)[b // 2][:, (b % 2) * P:(b % 2 + 1) * P])
         for b in range(4):
             parts = [slice(0, I)] if b < 3 else [slice(0, HALF), slice(HALF, I)]
             for n, cols in enumerate(parts):
@@ -149,4 +154,5 @@ def tile_list_picked_tokens_by_picked_classes_kernel(tc, xa_words, xa_scales, wc
                 res = keep.tile([P, width], F32, name=f"res{b}_{n}")
                 nc.vector.tensor_tensor(out=pre[:], in0=acc[b][:, cols], in1=bias[:, cols], op=ADD)
                 nc.scalar.activation(out=res[:], in_=pre[:], func=TANH)
-                nc.sync.dma_start(out=out[b * P:(b + 1) * P, cols], in_=res[:])
+                queue = nc.scalar if (b, n) == (3, 1) else nc.sync
+                queue.dma_start(out=out[b * P:(b + 1) * P, cols], in_=res[:])

@@ -30,12 +30,14 @@ def tile_list_picked_tokens_by_picked_classes_kernel(tc, xa_words, xa_scales, wc
         tok_list = keep.tile([P, J // 16], U16, name="tok_list")
         cls_list = keep.tile([P, I // 16], U16, name="cls_list")
         x_words = [keep.tile([P, T], I32, name=f"x_words{z}") for z in range(2)]
-        x_scales = keep.tile([P, T // 4], I32, name="x_scales")
+        x_scales = keep.tile([P, T // 4], I32, name="x_scales", tag="x_scales")
         cb_row = keep.tile([P, C], F32, name="cb_row")
         ident = keep.tile([P, P], F32, name="ident")
         warm = keep.tile([P, 8], F32, name="warm")
         warm_out = keep.tile([P, 8], F32, name="warm_out")
-        raw = [[keep.tile([P, 2, C // 2], F32, name=f"raw{q}_{h}", tag=f"raw{q}_{h}") for h in range(2)] for q in range(4)]
+        whole = keep.tile([P, 2, C], F32, name="whole")
+        raw = [[whole[:, :, h * (C // 2):(h + 1) * (C // 2)] if q == 1 else
+                keep.tile([P, 2, C // 2], F32, name=f"raw{q}_{h}", tag=f"raw{q}_{h}") for h in range(2)] for q in range(4)]
         pairs = [keep.tile([P, C], F32, name=f"pairs{q}") for q in range(4)]
 
         nc.gpsimd.memset(x_scales[:], 0)
@@ -54,13 +56,14 @@ def tile_list_picked_tokens_by_picked_classes_kernel(tc, xa_words, xa_scales, wc
         nc.sync.dma_start(cls_list[:], offs2)
         nc.sync.dma_start(tok_list[:], offs)
         nc.sync.dma_start(out=cb_row[P - 1:P, :], in_=cb[0:1, :])
-        load_wc(0, 0)
         load_x(0)
-        load_wc(0, 1)
+        load_wc(0, 0)
         sc32 = xa_scales.bitcast(I32)
         for quad in range(4):
             nc.sync.dma_start(out=x_scales[32 * quad:32 * quad + 8, :], in_=sc32[:, 4 * quad:4 * quad + 4, :])
-        for q in range(1, 4):
+        load_wc(0, 1)
+        nc.sync.dma_start(out=whole[:], in_=wc_rows[0, 1])
+        for q in range(2, 4):
             load_wc(q, 0)
             load_wc(q, 1)
         load_x(1)
@@ -81,9 +84,8 @@ def tile_list_picked_tokens_by_picked_classes_kernel(tc, xa_words, xa_scales, wc
         ws = [keep.tile([P, I], U8, name=f"ws{z}", align_bytes=64) for z in range(2)]
         cbg = keep.tile([P, I], F32, name="cbg")
         bcol = keep.tile([P, 4], F32, name="bcol")
-        g0 = keep.tile([P, 2, I], F32, name="g0")
         il0 = [keep.tile([P, HALF, 2], F32, name=f"il0_{h}", align_bytes=64) for h in range(2)]
-        g1 = [keep.tile([P, 2, HALF], F32, name=f"g1_{h}", tag=f"g1_{h}", align_bytes=64) for h in range(2)]
+        g1 = keep.tile([P, 2, I], F32, name="g1", tag="g1", align_bytes=64)
         il1 = [keep.tile([P, HALF, 2], F32, name=f"il1_{h}", align_bytes=64) for h in range(2)]
         acc = [psum.tile([P, I], F32, name=f"acc{b}") for b in range(4)]
         ps1 = psum.tile([P, 4, P], F32, name="ps1")
@@ -114,9 +116,10 @@ def tile_list_picked_tokens_by_picked_classes_kernel(tc, xa_words, xa_scales, wc
         nc.vector.tensor_copy(out=xg0[:], in_=x_words[0][:].bitcast(U32).indirect(tok_list[:]))
         nc.vector.tensor_copy(out=xsg[:], in_=x_scales[:].bitcast(U8).indirect(tok_list[:]))
         cast(0, 1, "scalar")
+        g0 = keep.tile([P, 2, I], F32, name="g0", tag="x_scales")
         nc.vector.tensor_copy(out=g0[:, 0, :], in_=pairs[0][:].indirect(cls_list[:]))
         cast(1, 0, "scalar")
-        cast(1, 1, "scalar")
+        cast(1, 1, "vector")
         nc.vector.tensor_copy(out=g0[:, 1, :], in_=pairs[1][:].indirect(cls_list[:]))
         for h in range(2):
             nc.vector.tensor_copy(out=il0[h][:], in_=g0[:, :, h * HALF:(h + 1) * HALF].rearrange("p u c -> p c u"))
@@ -128,26 +131,27 @@ def tile_list_picked_tokens_by_picked_classes_kernel(tc, xa_words, xa_scales, wc
             multiply(0, b, xg0[:, b * P:(b + 1) * P])
         cast(2, 0, "scalar")
         cast(2, 1, "scalar")
-        for h in range(2):
-            nc.vector.tensor_copy(out=g1[h][:, 0, :], in_=pairs[2][:].indirect(half_list(cls_list, h)))
+        nc.vector.tensor_copy(out=g1[:, 0, :], in_=pairs[2][:].indirect(cls_list[:]))
         cast(3, 0, "scalar")
-        cast(3, 1, "vector")
-        bias = keep.tile([P, I], F32, name="bias", tag="raw3_0")
+        cast(3, 1, "scalar", 0, 320)
+        cast(3, 1, "vector", 320, C // 2)
+        bias = keep.tile([P, I], F32, name="bias", tag="raw3_1")
         nc.scalar.copy(out=bias[:], in_=ps2[:])
         for h in range(2):
-            nc.vector.tensor_copy(out=g1[h][:, 1, :], in_=pairs[3][:].indirect(half_list(cls_list, h)))
-            nc.scalar.copy(out=il1[h][:], in_=g1[h][:].rearrange("p u c -> p c u"))
+            cols = slice(h * HALF, (h + 1) * HALF)
+            nc.vector.tensor_copy(out=g1[:, 1, cols], in_=pairs[3][:].indirect(half_list(cls_list, h)))
+            nc.scalar.copy(out=il1[h][:], in_=g1[:, :, cols].rearrange("p u c -> p c u"))
         nc.vector.tensor_copy(out=xg1a[:], in_=x_words[1][:].bitcast(U32).indirect(half_list(tok_list, 0)))
         for h in range(2):
             cols = slice(h * HALF, (h + 1) * HALF)
             nc.vector.quantize_mx(out=wq[1][:, cols].bitcast(FP8X4), scales=ws[1][:, cols],
                                   in_=il1[h][:].rearrange("p c u -> p (c u)").bitcast(BF16))
-        xg1b = keep.tile([P, HALF], U32, name="xg1b", tag="g1_1", align_bytes=64)
+        xg1b = keep.tile([P, HALF], U32, name="xg1b", tag="g1", align_bytes=64)
         nc.vector.tensor_copy(out=xg1b[:], in_=x_words[1][:].bitcast(U32).indirect(half_list(tok_list, 1)))
         for b in range(4):
             multiply(1, b, (xg1a, xg1b)[b // 2][:, (b % 2) * P:(b % 2 + 1) * P])
         for b in range(4):
-            parts = [slice(0, I)] if b < 3 else [slice(0, HALF), slice(HALF, I)]
+            parts = {0: [slice(0, P), slice(P, I)], 3: [slice(0, HALF), slice(HALF, I)]}.get(b, [slice(0, I)])
             for n, cols in enumerate(parts):
                 width = cols.stop - cols.start
                 pre = keep.tile([P, width], F32, name=f"pre{b}_{n}")

@@ -18,7 +18,13 @@ ADD = mybir.AluOpType.add
 TANH = mybir.ActivationFunctionType.Tanh
 
 P = 128
+BLOCKS = J // P
+PASSES = K // 512
+PAIRS = 2 * PASSES
+CHUNK = C // 2
 HALF = 256
+BIAS_ROW = P - 1
+SCALAR_SHARE = (320, 192, CHUNK, 256)
 
 
 def tile_list_picked_tokens_by_picked_classes_kernel(tc, xa_words, xa_scales, wc, cb, offs, offs2, out):
@@ -29,134 +35,141 @@ def tile_list_picked_tokens_by_picked_classes_kernel(tc, xa_words, xa_scales, wc
 
         tok_list = keep.tile([P, J // 16], U16, name="tok_list")
         cls_list = keep.tile([P, I // 16], U16, name="cls_list")
-        x_words = [keep.tile([P, T], I32, name=f"x_words{z}") for z in range(2)]
+        x_words = [keep.tile([P, T], I32, name=f"x_words{z}") for z in range(PASSES)]
         x_scales = keep.tile([P, T // 4], I32, name="x_scales", tag="x_scales")
         cb_row = keep.tile([P, C], F32, name="cb_row")
         ident = keep.tile([P, P], F32, name="ident")
-        warm = keep.tile([P, 8], F32, name="warm")
-        warm_out = keep.tile([P, 8], F32, name="warm_out")
-        whole = keep.tile([P, 2, C], F32, name="whole")
-        raw = [[whole[:, :, h * (C // 2):(h + 1) * (C // 2)] if q == 1 else
-                keep.tile([P, 2, C // 2], F32, name=f"raw{q}_{h}", tag=f"raw{q}_{h}") for h in range(2)] for q in range(4)]
-        pairs = [keep.tile([P, C], F32, name=f"pairs{q}") for q in range(4)]
+        raw = [[keep.tile([P, 2, CHUNK], F32, name=f"raw{q}_{h}", tag=f"raw{q}_{h}") for h in range(2)]
+               for q in range(PAIRS)]
+        pairs = [keep.tile([P, C], F32, name=f"pairs{q}") for q in range(PAIRS)]
 
         nc.gpsimd.memset(x_scales[:], 0)
-        nc.vector.memset(warm[:], 0.0)
-        nc.vector.memset(cb_row[0:P - 1, :], 0.0)
-        nc.scalar.activation(out=warm_out[:], in_=warm[:], func=TANH)
+        nc.vector.memset(cb_row[0:BIAS_ROW, :], 0.0)
 
-        wc_rows = wc.rearrange("(z p u t) c -> z u p t c", z=2, u=2, t=2)
+        wc_rows = wc.rearrange("(z p u t) c -> z u p t c", z=PASSES, u=2, t=2)
 
         def load_wc(q, h):
-            nc.sync.dma_start(out=raw[q][h][:], in_=wc_rows[q // 2, q % 2][:, :, h * (C // 2):(h + 1) * (C // 2)])
+            nc.sync.dma_start(out=raw[q][h][:], in_=wc_rows[q // 2, q % 2][:, :, h * CHUNK:(h + 1) * CHUNK])
 
         def load_x(z):
             nc.sync.dma_start(out=x_words[z][:], in_=xa_words[z].rearrange("p n t -> p (n t)").bitcast(I32))
 
         nc.sync.dma_start(cls_list[:], offs2)
-        nc.sync.dma_start(tok_list[:], offs)
-        nc.sync.dma_start(out=cb_row[P - 1:P, :], in_=cb[0:1, :])
+        nc.scalar.dma_start(out=cb_row[BIAS_ROW:P, :], in_=cb[0:1, :])
         load_x(0)
+        nc.sync.dma_start(tok_list[:], offs)
         load_wc(0, 0)
-        sc32 = xa_scales.bitcast(I32)
+        scale_rows = xa_scales.bitcast(I32)
         for quad in range(4):
-            nc.sync.dma_start(out=x_scales[32 * quad:32 * quad + 8, :], in_=sc32[:, 4 * quad:4 * quad + 4, :])
+            nc.sync.dma_start(out=x_scales[32 * quad:32 * quad + 8, :], in_=scale_rows[:, 4 * quad:4 * quad + 4, :])
         load_wc(0, 1)
-        nc.sync.dma_start(out=whole[:], in_=wc_rows[0, 1])
-        for q in range(2, 4):
+        for q in range(1, PAIRS):
             load_wc(q, 0)
             load_wc(q, 1)
         load_x(1)
         make_identity(nc, ident[:])
 
-        def cast(q, h, eng, lo=0, hi=C // 2):
-            dst = pairs[q][:].bitcast(BF16).rearrange("p (c t) -> p c t", t=2)[:, h * (C // 2) + lo:h * (C // 2) + hi, :]
-            src = raw[q][h][:, :, lo:hi].rearrange("p t c -> p c t")
-            if eng == "scalar":
-                nc.scalar.copy(out=dst, in_=src)
-            else:
-                nc.vector.tensor_copy(out=dst, in_=src)
+        def cast(copy, q, h, lo, hi):
+            dst = pairs[q][:].bitcast(BF16).rearrange("p (c t) -> p c t", t=2)
+            copy(out=dst[:, h * CHUNK + lo:h * CHUNK + hi, :], in_=raw[q][h][:, :, lo:hi].rearrange("p t c -> p c t"))
 
-        xg0 = keep.tile([P, J], U32, name="xg0", align_bytes=64)
-        xg1a = keep.tile([P, HALF], U32, name="xg1a", align_bytes=64)
-        xsg = keep.tile([P, J], U8, name="xsg", align_bytes=64)
-        wq = [keep.tile([P, I], U32, name=f"wq{z}", align_bytes=64) for z in range(2)]
-        ws = [keep.tile([P, I], U8, name=f"ws{z}", align_bytes=64) for z in range(2)]
-        cbg = keep.tile([P, I], F32, name="cbg")
-        bcol = keep.tile([P, 4], F32, name="bcol")
-        il0 = [keep.tile([P, HALF, 2], F32, name=f"il0_{h}", align_bytes=64) for h in range(2)]
-        g1 = keep.tile([P, 2, I], F32, name="g1", tag="g1", align_bytes=64)
-        il1 = [keep.tile([P, HALF, 2], F32, name=f"il1_{h}", align_bytes=64) for h in range(2)]
-        acc = [psum.tile([P, I], F32, name=f"acc{b}") for b in range(4)]
-        ps1 = psum.tile([P, 4, P], F32, name="ps1")
-        ps2 = psum.tile([P, I], F32, name="ps2")
+        def cast_first_chunk(q):
+            cast(nc.scalar.copy, q, 0, 0, CHUNK)
+
+        def cast_second_chunk(q):
+            cast(nc.scalar.copy, q, 1, 0, SCALAR_SHARE[q])
+            if SCALAR_SHARE[q] < CHUNK:
+                cast(nc.vector.tensor_copy, q, 1, SCALAR_SHARE[q], CHUNK)
+
+        def half_cols(h):
+            return slice(h * HALF, (h + 1) * HALF)
 
         def half_list(lst, h):
             return lst[:, h * (HALF // 16):(h + 1) * (HALF // 16)]
 
-        def multiply(z, b, words):
-            cols = slice(b * P, (b + 1) * P)
+        x0_picked = keep.tile([P, J], U32, name="x0_picked", align_bytes=64)
+        x1_picked_lo = keep.tile([P, HALF], U32, name="x1_picked_lo", align_bytes=64)
+        x_scales_picked = keep.tile([P, J], U8, name="x_scales_picked", align_bytes=64)
+        w_codes = [keep.tile([P, I], U32, name=f"w_codes{z}", align_bytes=64) for z in range(PASSES)]
+        w_scales = [keep.tile([P, I], U8, name=f"w_scales{z}", align_bytes=64) for z in range(PASSES)]
+        cb_picked = keep.tile([P, I], F32, name="cb_picked")
+        bias_cols = keep.tile([P, BLOCKS], F32, name="bias_cols")
+        woven0 = [keep.tile([P, HALF, 2], F32, name=f"woven0_{h}", align_bytes=64) for h in range(2)]
+        picked1 = keep.tile([P, 2, I], F32, name="picked1", tag="picked1", align_bytes=64)
+        woven1 = [keep.tile([P, HALF, 2], F32, name=f"woven1_{h}", align_bytes=64) for h in range(2)]
+        acc = [psum.tile([P, I], F32, name=f"acc{b}") for b in range(BLOCKS)]
+        bias_turned = psum.tile([P, BLOCKS, P], F32, name="bias_turned")
+        bias_spread = psum.tile([P, I], F32, name="bias_spread")
+
+        def weave(copy, woven, picked, h):
+            copy(out=woven[:], in_=picked[:, :, half_cols(h)].rearrange("p u c -> p c u"))
+
+        def quantise(z, woven, h):
+            nc.vector.quantize_mx(out=w_codes[z][:, half_cols(h)].bitcast(FP8X4), scales=w_scales[z][:, half_cols(h)],
+                                  in_=woven[:].rearrange("p c u -> p (c u)").bitcast(BF16))
+
+        def multiply(z, b, words, cols, stop):
             nc.tensor.matmul_mx(
-                out=acc[b][:],
+                out=acc[b][:, cols],
                 lhsT=words.bitcast(FP8X4),
-                lhsT_scale=xsg[4 * z:P, cols],
-                rhs=wq[z][:].bitcast(FP8X4),
-                rhs_scale=ws[z][:],
+                lhsT_scale=x_scales_picked[4 * z:P, b * P:(b + 1) * P],
+                rhs=w_codes[z][:, cols].bitcast(FP8X4),
+                rhs_scale=w_scales[z][:, cols],
                 start=(z == 0),
-                stop=(z == 1),
+                stop=stop,
             )
 
-        nc.vector.tensor_copy(out=cbg[:], in_=cb_row[:].indirect(cls_list[:]))
-        cast(0, 0, "scalar")
-        for b in range(4):
-            nc.tensor.transpose(ps1[:, b, :], cbg[:, b * P:(b + 1) * P], ident[:])
-        nc.vector.tensor_copy(out=bcol[:], in_=ps1[:, :, P - 1])
-        for b in range(4):
-            nc.tensor.transpose(ps2[:, b * P:(b + 1) * P], bcol[:, b:b + 1].to_broadcast([P, P]), ident[:])
-        nc.vector.tensor_copy(out=xg0[:], in_=x_words[0][:].bitcast(U32).indirect(tok_list[:]))
-        nc.vector.tensor_copy(out=xsg[:], in_=x_scales[:].bitcast(U8).indirect(tok_list[:]))
-        cast(0, 1, "scalar")
-        g0 = keep.tile([P, 2, I], F32, name="g0", tag="x_scales")
-        nc.vector.tensor_copy(out=g0[:, 0, :], in_=pairs[0][:].indirect(cls_list[:]))
-        cast(1, 0, "scalar")
-        cast(1, 1, "vector")
-        nc.vector.tensor_copy(out=g0[:, 1, :], in_=pairs[1][:].indirect(cls_list[:]))
+        nc.vector.tensor_copy(out=cb_picked[:], in_=cb_row[:].indirect(cls_list[:]))
+        cast_first_chunk(0)
+        for b in range(BLOCKS):
+            nc.tensor.transpose(bias_turned[:, b, :], cb_picked[:, b * P:(b + 1) * P], ident[:])
+        nc.vector.tensor_copy(out=bias_cols[:], in_=bias_turned[:, :, BIAS_ROW])
+        for b in range(BLOCKS):
+            nc.tensor.transpose(bias_spread[:, b * P:(b + 1) * P], bias_cols[:, b:b + 1].to_broadcast([P, P]), ident[:])
+
+        nc.vector.tensor_copy(out=x0_picked[:], in_=x_words[0][:].bitcast(U32).indirect(tok_list[:]))
+        nc.vector.tensor_copy(out=x_scales_picked[:], in_=x_scales[:].bitcast(U8).indirect(tok_list[:]))
+        cast_second_chunk(0)
+        picked0 = keep.tile([P, 2, I], F32, name="picked0", tag="x_scales")
+        nc.vector.tensor_copy(out=picked0[:, 0, :], in_=pairs[0][:].indirect(cls_list[:]))
+        cast_first_chunk(1)
+        cast_second_chunk(1)
+        nc.vector.tensor_copy(out=picked0[:, 1, :], in_=pairs[1][:].indirect(cls_list[:]))
         for h in range(2):
-            nc.vector.tensor_copy(out=il0[h][:], in_=g0[:, :, h * HALF:(h + 1) * HALF].rearrange("p u c -> p c u"))
+            weave(nc.vector.tensor_copy, woven0[h], picked0, h)
         for h in range(2):
-            cols = slice(h * HALF, (h + 1) * HALF)
-            nc.vector.quantize_mx(out=wq[0][:, cols].bitcast(FP8X4), scales=ws[0][:, cols],
-                                  in_=il0[h][:].rearrange("p c u -> p (c u)").bitcast(BF16))
-        for b in range(4):
-            multiply(0, b, xg0[:, b * P:(b + 1) * P])
-        cast(2, 0, "scalar")
-        cast(2, 1, "scalar")
-        nc.vector.tensor_copy(out=g1[:, 0, :], in_=pairs[2][:].indirect(cls_list[:]))
-        cast(3, 0, "scalar")
-        cast(3, 1, "scalar", 0, 320)
-        cast(3, 1, "vector", 320, C // 2)
+            quantise(0, woven0[h], h)
+        for b in range(BLOCKS):
+            multiply(0, b, x0_picked[:, b * P:(b + 1) * P], slice(0, I), stop=False)
+
+        cast_first_chunk(2)
+        cast_second_chunk(2)
+        nc.vector.tensor_copy(out=picked1[:, 0, :], in_=pairs[2][:].indirect(cls_list[:]))
+        cast_first_chunk(3)
+        cast_second_chunk(3)
         bias = keep.tile([P, I], F32, name="bias", tag="raw3_1")
-        nc.scalar.copy(out=bias[:], in_=ps2[:])
+        nc.scalar.copy(out=bias[:], in_=bias_spread[:])
         for h in range(2):
-            cols = slice(h * HALF, (h + 1) * HALF)
-            nc.vector.tensor_copy(out=g1[:, 1, cols], in_=pairs[3][:].indirect(half_list(cls_list, h)))
-            nc.scalar.copy(out=il1[h][:], in_=g1[:, :, cols].rearrange("p u c -> p c u"))
-        nc.vector.tensor_copy(out=xg1a[:], in_=x_words[1][:].bitcast(U32).indirect(half_list(tok_list, 0)))
+            nc.vector.tensor_copy(out=picked1[:, 1, half_cols(h)], in_=pairs[3][:].indirect(half_list(cls_list, h)))
+            weave(nc.scalar.copy, woven1[h], picked1, h)
+        nc.vector.tensor_copy(out=x1_picked_lo[:], in_=x_words[1][:].bitcast(U32).indirect(half_list(tok_list, 0)))
         for h in range(2):
-            cols = slice(h * HALF, (h + 1) * HALF)
-            nc.vector.quantize_mx(out=wq[1][:, cols].bitcast(FP8X4), scales=ws[1][:, cols],
-                                  in_=il1[h][:].rearrange("p c u -> p (c u)").bitcast(BF16))
-        xg1b = keep.tile([P, HALF], U32, name="xg1b", tag="g1", align_bytes=64)
-        nc.vector.tensor_copy(out=xg1b[:], in_=x_words[1][:].bitcast(U32).indirect(half_list(tok_list, 1)))
-        for b in range(4):
-            multiply(1, b, (xg1a, xg1b)[b // 2][:, (b % 2) * P:(b % 2 + 1) * P])
-        for b in range(4):
-            parts = {0: [slice(0, P), slice(P, I)], 3: [slice(0, HALF), slice(HALF, I)]}.get(b, [slice(0, I)])
-            for n, cols in enumerate(parts):
-                width = cols.stop - cols.start
-                pre = keep.tile([P, width], F32, name=f"pre{b}_{n}")
-                res = keep.tile([P, width], F32, name=f"res{b}_{n}")
-                nc.vector.tensor_tensor(out=pre[:], in0=acc[b][:, cols], in1=bias[:, cols], op=ADD)
-                nc.scalar.activation(out=res[:], in_=pre[:], func=TANH)
-                queue = nc.scalar if (b, n) == (3, 1) else nc.sync
-                queue.dma_start(out=out[b * P:(b + 1) * P, cols], in_=res[:])
+            quantise(1, woven1[h], h)
+            for b in range(BLOCKS // 2):
+                multiply(1, b, x1_picked_lo[:, b * P:(b + 1) * P], half_cols(h), stop=(h == 1))
+        x1_picked_hi = keep.tile([P, HALF], U32, name="x1_picked_hi", tag="picked1", align_bytes=64)
+        nc.vector.tensor_copy(out=x1_picked_hi[:], in_=x_words[1][:].bitcast(U32).indirect(half_list(tok_list, 1)))
+        for b in range(BLOCKS // 2):
+            multiply(1, BLOCKS // 2 + b, x1_picked_hi[:, b * P:(b + 1) * P], slice(0, I), stop=True)
+
+        for b in range(BLOCKS):
+            rows = slice(b * P, (b + 1) * P)
+            result = keep.tile([P, I], F32, name=f"result{b}")
+            for h in range(2):
+                biased = keep.tile([P, HALF], F32, name=f"biased{b}_{h}")
+                nc.vector.tensor_tensor(out=biased[:], in0=acc[b][:, half_cols(h)], in1=bias[:, half_cols(h)], op=ADD)
+                nc.scalar.activation(out=result[:, half_cols(h)], in_=biased[:], func=TANH)
+                if b == BLOCKS - 1:
+                    (nc.sync, nc.scalar)[h].dma_start(out=out[rows, half_cols(h)], in_=result[:, half_cols(h)])
+            if b < BLOCKS - 1:
+                nc.sync.dma_start(out=out[rows, :], in_=result[:])

from contextlib import ExitStack

import concourse.mybir as mybir
from concourse.masks import make_identity

K, T, C, J, I = 1024, 1024, 1024, 512, 512
FLOPS = 2 * K * J * I
BYTES = K * T + K * T // 32 + 4 * K * C + 4 * C + 2 * 2 * 128 * 32 + 4 * J * I

F32 = mybir.dt.float32
BF16 = mybir.dt.bfloat16
I32 = mybir.dt.int32
U32 = mybir.dt.uint32
U16 = mybir.dt.uint16
U8 = mybir.dt.uint8
FP8X4 = mybir.dt.float8_e4m3fn_x4
ADD = mybir.AluOpType.add
TANH = mybir.ActivationFunctionType.Tanh

P = 128
BLOCKS = J // P
PASSES = K // 512
PAIRS = 2 * PASSES
CHUNK = C // 2
HALF = 256
BIAS_ROW = P - 1
SCALAR_SHARE = (320, 192, CHUNK, 256)


def tile_list_picked_tokens_by_picked_classes_kernel(tc, xa_words, xa_scales, wc, cb, offs, offs2, out):
    nc = tc.nc
    with ExitStack() as ctx:
        keep = ctx.enter_context(tc.tile_pool(name="keep", bufs=1))
        psum = ctx.enter_context(tc.psum_pool(name="psum", bufs=1))

        tok_list = keep.tile([P, J // 16], U16, name="tok_list")
        cls_list = keep.tile([P, I // 16], U16, name="cls_list")
        x_words = [keep.tile([P, T], I32, name=f"x_words{z}") for z in range(PASSES)]
        x_scales = keep.tile([P, T // 4], I32, name="x_scales", tag="x_scales")
        cb_row = keep.tile([P, C], F32, name="cb_row")
        ident = keep.tile([P, P], F32, name="ident")
        raw = [[keep.tile([P, 2, CHUNK], F32, name=f"raw{q}_{h}", tag=f"raw{q}_{h}") for h in range(2)]
               for q in range(PAIRS)]
        pairs = [keep.tile([P, C], F32, name=f"pairs{q}") for q in range(PAIRS)]

        nc.gpsimd.memset(x_scales[:], 0)
        nc.vector.memset(cb_row[0:BIAS_ROW, :], 0.0)

        wc_rows = wc.rearrange("(z p u t) c -> z u p t c", z=PASSES, u=2, t=2)

        def load_wc(q, h):
            nc.sync.dma_start(out=raw[q][h][:], in_=wc_rows[q // 2, q % 2][:, :, h * CHUNK:(h + 1) * CHUNK])

        def load_x(z):
            nc.sync.dma_start(out=x_words[z][:], in_=xa_words[z].rearrange("p n t -> p (n t)").bitcast(I32))

        nc.sync.dma_start(cls_list[:], offs2)
        nc.scalar.dma_start(out=cb_row[BIAS_ROW:P, :], in_=cb[0:1, :])
        load_x(0)
        nc.sync.dma_start(tok_list[:], offs)
        load_wc(0, 0)
        scale_rows = xa_scales.bitcast(I32)
        for quad in range(4):
            nc.sync.dma_start(out=x_scales[32 * quad:32 * quad + 8, :], in_=scale_rows[:, 4 * quad:4 * quad + 4, :])
        load_wc(0, 1)
        for q in range(1, PAIRS):
            load_wc(q, 0)
            load_wc(q, 1)
        load_x(1)
        make_identity(nc, ident[:])

        def cast(copy, q, h, lo, hi):
            dst = pairs[q][:].bitcast(BF16).rearrange("p (c t) -> p c t", t=2)
            copy(out=dst[:, h * CHUNK + lo:h * CHUNK + hi, :], in_=raw[q][h][:, :, lo:hi].rearrange("p t c -> p c t"))

        def cast_first_chunk(q):
            cast(nc.scalar.copy, q, 0, 0, CHUNK)

        def cast_second_chunk(q):
            cast(nc.scalar.copy, q, 1, 0, SCALAR_SHARE[q])
            if SCALAR_SHARE[q] < CHUNK:
                cast(nc.vector.tensor_copy, q, 1, SCALAR_SHARE[q], CHUNK)

        def half_cols(h):
            return slice(h * HALF, (h + 1) * HALF)

        def half_list(lst, h):
            return lst[:, h * (HALF // 16):(h + 1) * (HALF // 16)]

        x0_picked = keep.tile([P, J], U32, name="x0_picked", align_bytes=64)
        x1_picked_lo = keep.tile([P, HALF], U32, name="x1_picked_lo", align_bytes=64)
        x_scales_picked = keep.tile([P, J], U8, name="x_scales_picked", align_bytes=64)
        w_codes = [keep.tile([P, I], U32, name=f"w_codes{z}", align_bytes=64) for z in range(PASSES)]
        w_scales = [keep.tile([P, I], U8, name=f"w_scales{z}", align_bytes=64) for z in range(PASSES)]
        cb_picked = keep.tile([P, I], F32, name="cb_picked")
        bias_cols = keep.tile([P, BLOCKS], F32, name="bias_cols")
        woven0 = [keep.tile([P, HALF, 2], F32, name=f"woven0_{h}", align_bytes=64) for h in range(2)]
        picked1 = keep.tile([P, 2, I], F32, name="picked1", tag="picked1", align_bytes=64)
        woven1 = [keep.tile([P, HALF, 2], F32, name=f"woven1_{h}", align_bytes=64) for h in range(2)]
        acc = [psum.tile([P, I], F32, name=f"acc{b}") for b in range(BLOCKS)]
        bias_turned = psum.tile([P, BLOCKS, P], F32, name="bias_turned")
        bias_spread = psum.tile([P, I], F32, name="bias_spread")

        def weave(copy, woven, picked, h):
            copy(out=woven[:], in_=picked[:, :, half_cols(h)].rearrange("p u c -> p c u"))

        def quantise(z, woven, h):
            nc.vector.quantize_mx(out=w_codes[z][:, half_cols(h)].bitcast(FP8X4), scales=w_scales[z][:, half_cols(h)],
                                  in_=woven[:].rearrange("p c u -> p (c u)").bitcast(BF16))

        def multiply(z, b, words, cols, stop):
            nc.tensor.matmul_mx(
                out=acc[b][:, cols],
                lhsT=words.bitcast(FP8X4),
                lhsT_scale=x_scales_picked[4 * z:P, b * P:(b + 1) * P],
                rhs=w_codes[z][:, cols].bitcast(FP8X4),
                rhs_scale=w_scales[z][:, cols],
                start=(z == 0),
                stop=stop,
            )

        nc.vector.tensor_copy(out=cb_picked[:], in_=cb_row[:].indirect(cls_list[:]))
        cast_first_chunk(0)
        for b in range(BLOCKS):
            nc.tensor.transpose(bias_turned[:, b, :], cb_picked[:, b * P:(b + 1) * P], ident[:])
        nc.vector.tensor_copy(out=bias_cols[:], in_=bias_turned[:, :, BIAS_ROW])
        for b in range(BLOCKS):
            nc.tensor.transpose(bias_spread[:, b * P:(b + 1) * P], bias_cols[:, b:b + 1].to_broadcast([P, P]), ident[:])

        nc.vector.tensor_copy(out=x0_picked[:], in_=x_words[0][:].bitcast(U32).indirect(tok_list[:]))
        nc.vector.tensor_copy(out=x_scales_picked[:], in_=x_scales[:].bitcast(U8).indirect(tok_list[:]))
        cast_second_chunk(0)
        picked0 = keep.tile([P, 2, I], F32, name="picked0", tag="x_scales")
        nc.vector.tensor_copy(out=picked0[:, 0, :], in_=pairs[0][:].indirect(cls_list[:]))
        cast_first_chunk(1)
        cast_second_chunk(1)
        nc.vector.tensor_copy(out=picked0[:, 1, :], in_=pairs[1][:].indirect(cls_list[:]))
        for h in range(2):
            weave(nc.vector.tensor_copy, woven0[h], picked0, h)
        for h in range(2):
            quantise(0, woven0[h], h)
        for b in range(BLOCKS):
            multiply(0, b, x0_picked[:, b * P:(b + 1) * P], slice(0, I), stop=False)

        cast_first_chunk(2)
        cast_second_chunk(2)
        nc.vector.tensor_copy(out=picked1[:, 0, :], in_=pairs[2][:].indirect(cls_list[:]))
        cast_first_chunk(3)
        cast_second_chunk(3)
        bias = keep.tile([P, I], F32, name="bias", tag="raw3_1")
        nc.scalar.copy(out=bias[:], in_=bias_spread[:])
        for h in range(2):
            nc.vector.tensor_copy(out=picked1[:, 1, half_cols(h)], in_=pairs[3][:].indirect(half_list(cls_list, h)))
            weave(nc.scalar.copy, woven1[h], picked1, h)
        nc.vector.tensor_copy(out=x1_picked_lo[:], in_=x_words[1][:].bitcast(U32).indirect(half_list(tok_list, 0)))
        for h in range(2):
            quantise(1, woven1[h], h)
            for b in range(BLOCKS // 2):
                multiply(1, b, x1_picked_lo[:, b * P:(b + 1) * P], half_cols(h), stop=(h == 1))
        x1_picked_hi = keep.tile([P, HALF], U32, name="x1_picked_hi", tag="picked1", align_bytes=64)
        nc.vector.tensor_copy(out=x1_picked_hi[:], in_=x_words[1][:].bitcast(U32).indirect(half_list(tok_list, 1)))
        for b in range(BLOCKS // 2):
            multiply(1, BLOCKS // 2 + b, x1_picked_hi[:, b * P:(b + 1) * P], slice(0, I), stop=True)

        for b in range(BLOCKS):
            rows = slice(b * P, (b + 1) * P)
            result = keep.tile([P, I], F32, name=f"result{b}")
            for h in range(2):
                biased = keep.tile([P, HALF], F32, name=f"biased{b}_{h}")
                nc.vector.tensor_tensor(out=biased[:], in0=acc[b][:, half_cols(h)], in1=bias[:, half_cols(h)], op=ADD)
                nc.scalar.activation(out=result[:, half_cols(h)], in_=biased[:], func=TANH)
                if b == BLOCKS - 1:
                    (nc.sync, nc.scalar)[h].dma_start(out=out[rows, half_cols(h)], in_=result[:, half_cols(h)])
            if b < BLOCKS - 1:
                nc.sync.dma_start(out=out[rows, :], in_=result[:])
